import numpy as np
import ml_dtypes


def mxq(x, axis, fmt="e4m3"):
    dtype, down = {"e4m3": (ml_dtypes.float8_e4m3fn, 7), "e5m2": (ml_dtypes.float8_e5m2, 14)}[fmt]
    v = np.moveaxis(np.asarray(x, np.float32).astype(ml_dtypes.bfloat16).astype(np.float64), axis, -1)
    blocks = v.reshape(v.shape[:-1] + (-1, 32))
    amax = np.abs(blocks).max(-1, keepdims=True)
    byte = np.maximum(np.where(amax > 0, np.frexp(amax)[1] - 1 + 127, 0) - down, 1)
    scale = np.exp2(byte - 127.0)
    codes = (blocks / scale).astype(np.float32).astype(dtype).astype(np.float64)
    return np.moveaxis((codes * scale).reshape(v.shape), -1, axis)


WIDE = False


def mx_kscale(k):
    if not WIDE:
        return np.ones(k)
    levels = np.array([10, -10, 5, -5, 0])
    if k % 512:
        return np.exp2(np.random.permutation(np.resize(levels, k // 32))).repeat(32)
    a = np.empty((k // 512, 16))
    for p in range(k // 512):
        a[p, :8] = np.random.permutation(np.resize(levels, 8))
        for g in range(8):
            far = levels[np.abs(levels - a[p, g]) >= 10]
            a[p, g + 8] = far[np.random.randint(len(far))]
    return np.exp2(a.ravel()).repeat(32)


def f64(x):
    return np.asarray(x).astype(np.float64)


E2M1 = np.array([0.0, 0.5, 1.0, 1.5, 2.0, 3.0, 4.0, 6.0, -0.0, -0.5, -1.0, -1.5, -2.0, -3.0, -4.0, -6.0])


def pack_weight(w, fmt):
    k, n = w.shape
    w = f64(np.asarray(w, np.float32).astype(ml_dtypes.bfloat16)).reshape(k // 32, 32, n)
    amax = np.abs(w).max(1)
    if fmt == "e4m3":
        byte = np.frexp(amax)[1] - 1 + 127 - 7
    else:
        mant, ex = np.frexp(amax / 6.0)
        byte = np.where(mant > 0.5, ex, ex - 1) + 127
    byte = np.clip(np.where(amax > 0, byte, 1), 1, 254)
    scaled = (w * np.exp2(127.0 - byte)[:, None, :]).reshape(k, n).astype(np.float32)
    by_word = np.ascontiguousarray(scaled.reshape(k // 512, 128, 4, n).transpose(0, 1, 3, 2))
    if fmt == "e4m3":
        words = by_word.astype(ml_dtypes.float8_e4m3fn).view(np.uint8)
    else:
        c = by_word.astype(ml_dtypes.float4_e2m1fn).view(np.uint8) & 0xF
        words = (c[..., 0::2] | (c[..., 1::2] << 4)).reshape(k // 512, 128, 2 * n)
    return np.ascontiguousarray(words), np.ascontiguousarray(byte.astype(np.uint8).reshape(k // 512, 16, n))


def unpack_weight(words, scales, fmt):
    g, _, n = scales.shape
    words = np.ascontiguousarray(words).reshape(g, 128, n, -1)
    if fmt == "e4m3":
        vals = words.view(ml_dtypes.float8_e4m3fn).astype(np.float64)
    else:
        nib = np.empty((g, 128, n, 4), np.uint8)
        nib[..., 0::2] = words & 0xF
        nib[..., 1::2] = words >> 4
        vals = E2M1[nib]
    vals = vals * np.repeat(np.exp2(scales.astype(np.float64) - 127.0), 8, axis=1)[..., None]
    return vals.transpose(0, 1, 3, 2).reshape(g * 512, n)


def planes(y):
    n, m = y.shape
    v = y.astype(np.float32).astype(ml_dtypes.bfloat16).astype(np.float64).reshape(n // 32, 32, m)
    top = np.abs(v).max(1)
    byte = np.clip(np.where(top > 0, np.frexp(top)[1] - 1 + 127 - 7, 1), 1, 254)
    codes = (v * np.exp2(127.0 - byte)[:, None, :]).reshape(n, m).astype(np.float32).astype(ml_dtypes.float8_e4m3fn).view(np.uint8)
    words = codes.reshape(n // 512, 128, 4, m).transpose(0, 1, 3, 2)
    return np.ascontiguousarray(words), np.ascontiguousarray(byte.astype(np.uint8).reshape(n // 512, 16, m))


K, R, M, T = 2560, 512, 1024, 512


def setup_inputs():
    n = np.random.standard_normal
    s = mx_kscale(K)[:, None]
    u = mx_kscale(R)[:, None]
    p_w4 = pack_weight(n((K, M)) / np.sqrt(K) / s, "e2m1")
    return {
        "x": (n((K, T)) * s).astype(np.float32),
        "w4_words": p_w4[0],
        "w4_scales": p_w4[1],
        "down": (n((K, R)) / np.sqrt(K) / s * u.T).astype(np.float32),
        "up": (0.5 * n((R, M)) / np.sqrt(R) / u).astype(np.float32),
    }


def reference(x, w4_words, w4_scales, down, up):
    x_ = mxq(f64(x), 0, "e4m3")
    w4_ = unpack_weight(w4_words, w4_scales, "e2m1")
    down_ = mxq(f64(down), 0, "e4m3")
    up_ = mxq(f64(up), 0, "e4m3")
    h_ = mxq(down_.T @ x_, 0, "e4m3")
    y = x_.T @ w4_ + h_.T @ up_
    out_0 = np.maximum(y, 0.0) ** 2
    return (out_0,) + planes(out_0)

@@ -1,0 +1,314 @@
+from contextlib import ExitStack
+
+import concourse.mybir as mybir
+
+K, R, M, T = 2560, 512, 1024, 512
+FLOPS = 2 * (K * R * T + K * M * T + R * M * T)
+
+F32 = mybir.dt.float32
+BF16 = mybir.dt.bfloat16
+I32 = mybir.dt.int32
+U32 = mybir.dt.uint32
+U8 = mybir.dt.uint8
+FP8X4 = mybir.dt.float8_e4m3fn_x4
+FP4X4 = mybir.dt.float4_e2m1fn_x4
+ACT = mybir.ActivationFunctionType
+ALU = mybir.AluOpType
+
+P = 128
+PACK = 4
+K_PASS = P * PACK
+PASSES = K // K_PASS
+NB = 128
+BANKS = M // NB
+HALF = M // 2
+UP_W = 256
+
+
+def tile_mix_lowrank_tm_pl_relu2_kernel(tc, x, w4_words, w4_scales, down, up, out_0, out_1, out_2):
+    nc = tc.nc
+    with ExitStack() as ctx:
+        sb = ctx.enter_context(tc.tile_pool(name="sb", bufs=1))
+        ps = ctx.enter_context(tc.psum_pool(name="ps", bufs=1))
+        ctx.enter_context(tc.manual_schedule())
+
+        def tile(name, shape, dtype):
+            return sb.tile(shape, dtype, name=name, tag=name, align_bytes=64)
+
+        def bank(i, name):
+            return ps.tile([P, PACK, NB], F32, name=name, tag="bank%d" % i)
+
+        def cast(eng, out, in_):
+            if eng == "v":
+                nc.vector.tensor_copy(out=out, in_=in_)
+            else:
+                nc.scalar.activation(out=out, in_=in_, func=ACT.Copy)
+
+        def cast_dealt(dst, at, raw, width):
+            cut = (2 * width // 3) // 4 * 4
+            for eng, m0, m1 in (("v", 0, cut), ("s", cut, width)):
+                cast(eng, dst[:, :, at + m0:at + m1, :].rearrange("p t m k -> p m k t"),
+                     raw[:, :, PACK * m0:PACK * m1].rearrange("p k (m t) -> p m k t", t=PACK))
+
+        def cast_plain(eng, dst, raw, n0, n1):
+            cast(eng, dst[:, n0:n1, :].rearrange("p (c i) k -> p c k i", i=4), raw[:, :, n0:n1].rearrange("p k (c i) -> p c k i", i=4))
+
+        def quant(codes, scales, src):
+            nc.vector.quantize_mx(out=codes.bitcast(FP8X4), scales=scales, in_=src)
+
+        def load_rows(name, src, a, c0, c1):
+            raw = tile(name, [P, PACK, c1 - c0], F32)
+            nc.sync.dma_start(out=raw[:], in_=src[a * K_PASS:(a + 1) * K_PASS, c0:c1].rearrange("(p k) w -> p k w", k=PACK))
+            return raw
+
+        w_sc = [tile("w_sc%d" % h, [P, PASSES, HALF], U8) for h in range(2)]
+        w_cols = [(0, HALF), (HALF, HALF + UP_W), (HALF + UP_W, M)]
+        w_wd = [tile("w_wd%d" % i, [P, PASSES, 2 * (n1 - n0)], U8) for i, (n0, n1) in enumerate(w_cols)]
+        for h in range(2):
+            nc.vector.memset(w_sc[h][:].bitcast(I32), 0)
+
+        def load_w_scales(h, queue):
+            for q in range(4):
+                queue.dma_start(
+                    out=w_sc[h][32 * q:32 * q + 4, :, :].bitcast(I32),
+                    in_=w4_scales[:, 4 * q:4 * q + 4, h * HALF:(h + 1) * HALF].rearrange("a r n -> r a n").bitcast(I32),
+                )
+
+        def load_w_words(i):
+            nc.sync.dma_start(
+                out=w_wd[i][:].bitcast(I32),
+                in_=w4_words[:, :, 2 * w_cols[i][0]:2 * w_cols[i][1]].rearrange("a p b -> p a b").bitcast(I32),
+            )
+
+        x_cd = [tile("x_cd%d" % a, [P, T], U32) for a in range(PASSES)]
+        x_sc = [tile("x_sc%d" % a, [P, T], U8) for a in range(PASSES)]
+        d_cd = [tile("d_cd%d" % a, [P, R], U32) for a in range(PASSES)]
+        d_sc = [tile("d_sc%d" % a, [P, R], U8) for a in range(PASSES)]
+        h_cd = [tile("h_cd%d" % c, [P, P], U32) for c in range(PACK)]
+        h_sc = [tile("h_sc%d" % c, [P, P], U8) for c in range(PACK)]
+        u_cd = [tile("u_cd%d" % i, [P, UP_W], U32) for i in range(M // UP_W)]
+        u_sc = [tile("u_sc%d" % i, [P, UP_W], U8) for i in range(M // UP_W)]
+        o_cd = tile("o_cd", [P, M], U32)
+        o_sc = tile("o_sc", [P, M], U8)
+
+        last = PASSES - 1
+        x_raw = []
+        d_raw = []
+        for a in range(last):
+            x_raw.append(load_rows("x_raw%d" % a, x, a, 0, T))
+            if a == 0:
+                load_w_scales(0, nc.scalar)
+            d_raw.append(load_rows("d_raw%d" % a, down, a, 0, R))
+            if a == 0:
+                load_w_words(0)
+        x_last = [load_rows("x_last%d" % u, x, last, u * T // 2, (u + 1) * T // 2) for u in range(2)]
+        d_last = [load_rows("d_last%d" % u, down, last, u * R // 2, (u + 1) * R // 2) for u in range(2)]
+        load_w_scales(1, nc.sync)
+        load_w_words(1)
+        u_raw = []
+        for i in range(M // UP_W):
+            u_raw.append(load_rows("u_raw%d" % i, up, 0, i * UP_W, (i + 1) * UP_W))
+            if i == 1:
+                load_w_words(2)
+
+        h_ps = [bank(4 + c, "h_ps%d" % c) for c in range(PACK)]
+        y_ps = [bank(b, "y_ps%d" % b) for b in range(4)]
+
+        def col(j):
+            return slice(j * P, (j + 1) * P)
+
+        def h_pass(a):
+            for c in range(PACK):
+                for j in range(PACK):
+                    nc.tensor.matmul_mx(
+                        out=h_ps[c][:, j, :], lhsT=d_cd[a][:, col(j)].bitcast(FP8X4), lhsT_scale=d_sc[a][:, col(j)],
+                        rhs=x_cd[a][:, col(c)].bitcast(FP8X4), rhs_scale=x_sc[a][:, col(c)],
+                        start=(a == 0 and j == 0), stop=(a == last and j == PACK - 1),
+                    )
+
+        def y_base(b, a):
+            h, n0 = divmod(b * NB, HALF)
+            i = max(i for i in range(len(w_cols)) if w_cols[i][0] <= b * NB)
+            w0 = b * NB - w_cols[i][0]
+            for j in range(PACK):
+                nc.tensor.matmul_mx(
+                    out=y_ps[b][:, j, :], lhsT=x_cd[a][:, col(j)].bitcast(FP8X4), lhsT_scale=x_sc[a][:, col(j)],
+                    rhs=w_wd[i][:, a, 2 * w0:2 * (w0 + NB)].bitcast(FP4X4), rhs_scale=w_sc[h][:, a, n0:n0 + NB],
+                    start=(a == 0 and j == 0), stop=False,
+                )
+
+        def y_base_all(b):
+            y_ps.append(bank(b, "y_ps%d" % b))
+            for a in range(PASSES):
+                y_base(b, a)
+
+        def y_up(b):
+            i, n0 = divmod(b * NB, UP_W)
+            for j in range(PACK):
+                nc.tensor.matmul_mx(
+                    out=y_ps[b][:, j, :], lhsT=h_cd[j][:].bitcast(FP8X4), lhsT_scale=h_sc[j][:],
+                    rhs=u_cd[i][:, n0:n0 + NB].bitcast(FP8X4), rhs_scale=u_sc[i][:, n0:n0 + NB],
+                    start=False, stop=(j == PACK - 1),
+                )
+
+        def flat(t):
+            return t[:].rearrange("p t m k -> p (t m k)")
+
+        for a in range(last):
+            xg = tile("xg", [P, PACK, P, PACK], BF16)
+            cast_dealt(xg, 0, x_raw[a], P)
+            quant(x_cd[a][:], x_sc[a][:], flat(xg))
+            for b in range(4):
+                y_base(b, a)
+            dg = tile("dg", [P, PACK, P, PACK], BF16)
+            cast_dealt(dg, 0, d_raw[a], P)
+            if a < last - 1:
+                quant(d_cd[a][:], d_sc[a][:], flat(dg))
+                h_pass(a)
+
+        xg = tile("xg", [P, PACK, P, PACK], BF16)
+        cast_dealt(xg, 0, x_last[0], P // 2)
+        quant(d_cd[last - 1][:], d_sc[last - 1][:], flat(dg))
+        h_pass(last - 1)
+        cast_dealt(xg, P // 2, x_last[1], P // 2)
+        quant(x_cd[last][:], x_sc[last][:], flat(xg))
+        for b in range(4):
+            y_base(b, last)
+        for u in range(2):
+            g = tile("dl%d" % u, [P, PACK, P // 2, PACK], BF16)
+            cast_dealt(g, 0, d_last[u], P // 2)
+            for j in range(PACK):
+                cs = slice(j * P + u * P // 2, j * P + (u + 1) * P // 2)
+                quant(d_cd[last][:, cs], d_sc[last][:, cs], g[:, j].rearrange("p m k -> p (m k)"))
+        h_pass(last)
+
+        ug = [tile("ug%d" % i, [P, UP_W, PACK], BF16) for i in range(M // UP_W)]
+        hg = [tile("hg%d" % c, [P, P, PACK], BF16) for c in range(PACK)]
+
+        def flat3(t):
+            return t[:].rearrange("p n k -> p (n k)")
+
+        def h_out(eng, c):
+            cast(eng, hg[c][:], h_ps[c][:].rearrange("p j t -> p t j"))
+
+        def h_quant(c):
+            quant(h_cd[c][:], h_sc[c][:], flat3(hg[c]))
+
+        def u_quant(i):
+            quant(u_cd[i][:], u_sc[i][:], flat3(ug[i]))
+
+        out0 = out_0.rearrange("(p j) n -> p j n", j=PACK)
+        out1 = out_1.rearrange("a p n i -> p (a n i)").bitcast(I32)
+        rl = {}
+        sq = {}
+        og = {}
+
+        for b in range(BANKS):
+            rl[b] = tile("rl%d" % b, [P, PACK, NB], F32)
+            sq[b] = tile("sq%d" % b, [P, PACK, NB], F32)
+            og[b] = tile("og%d" % b, [P, NB, PACK], BF16)
+
+        def relu(eng, b, n0=0, n1=NB):
+            if eng == "v":
+                nc.vector.tensor_scalar(out=rl[b][:, :, n0:n1], in0=y_ps[b][:, :, n0:n1], scalar1=0.0, scalar2=None, op0=ALU.max)
+            else:
+                nc.scalar.activation(out=rl[b][:, :, n0:n1], in_=y_ps[b][:, :, n0:n1], func=ACT.Relu)
+
+        def square(eng, b, n0=0, n1=NB):
+            if eng == "v":
+                nc.vector.tensor_tensor(out=sq[b][:, :, n0:n1], in0=rl[b][:, :, n0:n1], in1=rl[b][:, :, n0:n1], op=ALU.mult)
+            else:
+                nc.scalar.activation(out=sq[b][:, :, n0:n1], in_=rl[b][:, :, n0:n1], func=ACT.Square)
+
+        def store_out(b):
+            nc.sync.dma_start(out=out0[:, :, b * NB:(b + 1) * NB], in_=sq[b][:])
+
+        def o_cast(b, n0=0, n1=NB):
+            cast_plain("v", og[b], sq[b], n0, n1)
+
+        def o_quant(b):
+            quant(o_cd[:, b * NB:(b + 1) * NB], o_sc[:, b * NB:(b + 1) * NB], flat3(og[b]))
+
+        def u_cast(eng, i):
+            cast_plain(eng, ug[i], u_raw[i], 0, UP_W)
+
+        def store_codes(b0, b1):
+            nc.sync.dma_start(out=out1[:, b0 * NB:b1 * NB], in_=o_cd[:, b0 * NB:b1 * NB].bitcast(I32))
+
+        h_out("s", 0)
+        h_out("v", 1)
+        h_out("s", 2)
+        u_cast("v", 0)
+        h_out("s", 3)
+        h_quant(0)
+        h_quant(1)
+        u_quant(0)
+        h_quant(2)
+        h_quant(3)
+        u_cast("s", 1)
+        y_base_all(4)
+        y_up(0)
+        y_up(1)
+        relu("v", 0)
+        u_quant(1)
+        y_base_all(5)
+        y_up(2)
+        y_up(3)
+        relu("s", 1)
+        square("s", 0)
+        store_out(0)
+        u_cast("v", 2)
+        square("s", 1)
+        store_out(1)
+        o_cast(0)
+        u_quant(2)
+        y_up(4)
+        y_up(5)
+        o_quant(0)
+        relu("s", 2)
+        u_cast("v", 3)
+        relu("v", 3)
+        u_quant(3)
+        relu("s", 4)
+        square("s", 2)
+        store_out(2)
+        o_cast(1)
+        square("s", 3)
+        store_out(3)
+        y_base_all(6)
+        y_up(6)
+        y_base_all(7)
+        y_up(7)
+        relu("s", 5)
+        o_cast(2)
+        o_quant(1)
+        square("s", 4)
+        store_out(4)
+        o_cast(3)
+        o_quant(2)
+        square("s", 5)
+        store_out(5)
+        relu("v", 6)
+        o_quant(3)
+        store_codes(0, 4)
+        o_cast(4)
+        square("s", 6)
+        store_out(6)
+        o_cast(5)
+        o_quant(4)
+        o_quant(5)
+        store_codes(4, 6)
+        relu("s", 7, 0, 64)
+        relu("s", 7, 64, NB)
+        square("v", 7, 0, 64)
+        o_cast(6)
+        square("s", 7, 64, NB)
+        store_out(7)
+        o_cast(7, 0, 64)
+        o_cast(7, 64, NB)
+        o_quant(6)
+        o_quant(7)
+        store_codes(6, 8)
+        for q in range(4):
+            queue = nc.scalar if q % 2 else nc.sync
+            queue.dma_start(out=out_2[0, 4 * q:4 * q + 4, :].bitcast(I32), in_=o_sc[32 * q:32 * q + 4, :].bitcast(I32))

@@ -68,10 +68,10 @@ def tile_mix_lowrank_tm_pl_relu2_kernel(tc, x, w4_words, w4_scales, down, up, ou
             nc.vector.memset(w_sc[h][:].bitcast(I32), 0)
 
         def load_w_scales(h, queue):
-            for q in range(4):
+            for r in range(4):
                 queue.dma_start(
-                    out=w_sc[h][32 * q:32 * q + 4, :, :].bitcast(I32),
-                    in_=w4_scales[:, 4 * q:4 * q + 4, h * HALF:(h + 1) * HALF].rearrange("a r n -> r a n").bitcast(I32),
+                    out=w_sc[h][r:P:32, :, :].bitcast(I32),
+                    in_=w4_scales[:, r:16:4, h * HALF:(h + 1) * HALF].rearrange("a q n -> q a n").bitcast(I32),
                 )
 
         def load_w_words(i):
@@ -137,10 +137,12 @@ def tile_mix_lowrank_tm_pl_relu2_kernel(tc, x, w4_words, w4_scales, down, up, ou
                     start=(a == 0 and j == 0), stop=False,
                 )
 
-        def y_base_all(b):
-            y_ps.append(bank(b, "y_ps%d" % b))
-            for a in range(PASSES):
-                y_base(b, a)
+        def late_base(s0, s1):
+            for s in range(s0, s1):
+                b, a = divmod(s, PASSES)
+                if a == 0:
+                    y_ps.append(bank(4 + b, "y_ps%d" % (4 + b)))
+                y_base(4 + b, a)
 
         def y_up(b):
             i, n0 = divmod(b * NB, UP_W)
@@ -229,8 +231,17 @@ def tile_mix_lowrank_tm_pl_relu2_kernel(tc, x, w4_words, w4_scales, down, up, ou
         def o_quant(b):
             quant(o_cd[:, b * NB:(b + 1) * NB], o_sc[:, b * NB:(b + 1) * NB], flat3(og[b]))
 
-        def u_cast(eng, i):
-            cast_plain(eng, ug[i], u_raw[i], 0, UP_W)
+        def u_cast(i, shared):
+            cut = (2 * UP_W // 3) // 8 * 8 if shared else UP_W
+            cast_plain("v", ug[i], u_raw[i], 0, cut)
+            if shared:
+                cast_plain("s", ug[i], u_raw[i], cut, UP_W)
+
+        def store_scales(b0, b1, queues):
+            for r in range(4):
+                queues[r % len(queues)].dma_start(
+                    out=out_2[0, r:16:4, b0 * NB:b1 * NB].bitcast(I32),
+                    in_=o_sc[r:P:32, b0 * NB:b1 * NB].bitcast(I32))
 
         def store_codes(b0, b1):
             nc.sync.dma_start(out=out1[:, b0 * NB:b1 * NB], in_=o_cd[:, b0 * NB:b1 * NB].bitcast(I32))
@@ -238,77 +249,76 @@ def tile_mix_lowrank_tm_pl_relu2_kernel(tc, x, w4_words, w4_scales, down, up, ou
         h_out("s", 0)
         h_out("v", 1)
         h_out("s", 2)
-        u_cast("v", 0)
         h_out("s", 3)
-        h_quant(0)
-        h_quant(1)
+        for c in range(PACK - 1):
+            h_quant(c)
+        u_cast(0, True)
+        h_quant(PACK - 1)
         u_quant(0)
-        h_quant(2)
-        h_quant(3)
-        u_cast("s", 1)
-        y_base_all(4)
+        late_base(0, 6)
         y_up(0)
         y_up(1)
-        relu("v", 0)
+        u_cast(1, True)
+        relu("s", 0)
         u_quant(1)
-        y_base_all(5)
+        relu("v", 1)
+        late_base(6, 10)
         y_up(2)
         y_up(3)
-        relu("s", 1)
         square("s", 0)
         store_out(0)
-        u_cast("v", 2)
         square("s", 1)
         store_out(1)
+        u_cast(2, False)
         o_cast(0)
         u_quant(2)
+        relu("s", 2)
+        relu("s", 3)
+        late_base(10, 13)
         y_up(4)
         y_up(5)
-        o_quant(0)
-        relu("s", 2)
-        u_cast("v", 3)
-        relu("v", 3)
+        u_cast(3, False)
+        o_cast(1)
         u_quant(3)
-        relu("s", 4)
+        late_base(13, 15)
+        y_up(6)
+        late_base(15, 20)
+        y_up(7)
         square("s", 2)
         store_out(2)
-        o_cast(1)
         square("s", 3)
         store_out(3)
-        y_base_all(6)
-        y_up(6)
-        y_base_all(7)
-        y_up(7)
+        relu("v", 4)
         relu("s", 5)
+        o_quant(0)
         o_cast(2)
         o_quant(1)
         square("s", 4)
         store_out(4)
-        o_cast(3)
-        o_quant(2)
         square("s", 5)
         store_out(5)
-        relu("v", 6)
+        o_cast(3)
+        o_quant(2)
+        o_cast(4)
         o_quant(3)
         store_codes(0, 4)
-        o_cast(4)
-        square("s", 6)
-        store_out(6)
+        relu("s", 6)
         o_cast(5)
         o_quant(4)
+        end = 7
+        relu("s", end, 0, 64)
+        square("s", 6)
+        store_out(6)
+        relu("s", end, 64, NB)
+        square("v", end, 0, 64)
         o_quant(5)
-        store_codes(4, 6)
-        relu("s", 7, 0, 64)
-        relu("s", 7, 64, NB)
-        square("v", 7, 0, 64)
         o_cast(6)
-        square("s", 7, 64, NB)
-        store_out(7)
-        o_cast(7, 0, 64)
-        o_cast(7, 64, NB)
+        square("s", end, 64, NB)
+        store_out(end)
+        o_cast(end, 0, 64)
         o_quant(6)
-        o_quant(7)
-        store_codes(6, 8)
-        for q in range(4):
-            queue = nc.scalar if q % 2 else nc.sync
-            queue.dma_start(out=out_2[0, 4 * q:4 * q + 4, :].bitcast(I32), in_=o_sc[32 * q:32 * q + 4, :].bitcast(I32))
+        o_cast(end, 64, NB)
+        store_codes(4, 7)
+        o_quant(end)
+        store_codes(7, 8)
+        store_scales(0, 8, [nc.scalar, nc.sync])

@@ -47,11 +47,11 @@ def tile_mix_lowrank_tm_pl_relu2_kernel(tc, x, w4_words, w4_scales, down, up, ou
         def cast_dealt(dst, at, raw, width):
             cut = (2 * width // 3) // 4 * 4
             for eng, m0, m1 in (("v", 0, cut), ("s", cut, width)):
-                cast(eng, dst[:, :, at + m0:at + m1, :].rearrange("p t m k -> p m k t"),
-                     raw[:, :, PACK * m0:PACK * m1].rearrange("p k (m t) -> p m k t", t=PACK))
+                cast(eng, dst[:, :, at + m0:at + m1, :].rearrange("p t m k -> p m t k"),
+                     raw[:, :, PACK * m0:PACK * m1].rearrange("p k (m t) -> p m t k", t=PACK))
 
         def cast_plain(eng, dst, raw, n0, n1):
-            cast(eng, dst[:, n0:n1, :].rearrange("p (c i) k -> p c k i", i=4), raw[:, :, n0:n1].rearrange("p k (c i) -> p c k i", i=4))
+            cast(eng, dst[:, n0:n1, :], raw[:, :, n0:n1].rearrange("p k n -> p n k"))
 
         def quant(codes, scales, src):
             nc.vector.quantize_mx(out=codes.bitcast(FP8X4), scales=scales, in_=src)

@@ -19,306 +19,304 @@ P = 128
 PACK = 4
 K_PASS = P * PACK
 PASSES = K // K_PASS
-NB = 128
-BANKS = M // NB
-HALF = M // 2
-UP_W = 256
+LAST_PASS = PASSES - 1
+QUADRANT = 32
+SCALE_ROWS = K_PASS // 32
+CHUNK = 128
+CHUNKS = M // CHUNK
+EARLY = 4
+LAST_CHUNK = CHUNKS - 1
+UP_PIECE = 2 * CHUNK
+W_RANGES = ((0, EARLY * CHUNK), (EARLY * CHUNK, (EARLY + 2) * CHUNK), ((EARLY + 2) * CHUNK, M))
+LEAD = (6, 9, 11)
+VECTOR, SCALAR = "vector", "scalar"
+
+
+def vector_share(total, multiple):
+    return 2 * total // 3 // multiple * multiple
 
 
 def tile_mix_lowrank_tm_pl_relu2_kernel(tc, x, w4_words, w4_scales, down, up, out_0, out_1, out_2):
     nc = tc.nc
     with ExitStack() as ctx:
-        sb = ctx.enter_context(tc.tile_pool(name="sb", bufs=1))
-        ps = ctx.enter_context(tc.psum_pool(name="ps", bufs=1))
+        sbuf = ctx.enter_context(tc.tile_pool(name="sbuf", bufs=1))
+        psum = ctx.enter_context(tc.psum_pool(name="psum", bufs=1))
         ctx.enter_context(tc.manual_schedule())
 
-        def tile(name, shape, dtype):
-            return sb.tile(shape, dtype, name=name, tag=name, align_bytes=64)
+        def sb(name, shape, dtype):
+            return sbuf.tile(shape, dtype, name=name, tag=name, align_bytes=64)
 
-        def bank(i, name):
-            return ps.tile([P, PACK, NB], F32, name=name, tag="bank%d" % i)
+        def bank(number, name, shape):
+            return psum.tile(shape, F32, name=name, tag="bank%d" % number)
 
-        def cast(eng, out, in_):
-            if eng == "v":
+        def mx_tiles(name, count, width):
+            return [(sb("%s_words%d" % (name, i), [P, width], U32), sb("%s_scales%d" % (name, i), [P, width], U8)) for i in range(count)]
+
+        def span(i, width):
+            return slice(i * width, (i + 1) * width)
+
+
+        def round_copy(engine, out, in_):
+            if engine == VECTOR:
                 nc.vector.tensor_copy(out=out, in_=in_)
             else:
                 nc.scalar.activation(out=out, in_=in_, func=ACT.Copy)
 
-        def cast_dealt(dst, at, raw, width):
-            cut = (2 * width // 3) // 4 * 4
-            for eng, m0, m1 in (("v", 0, cut), ("s", cut, width)):
-                cast(eng, dst[:, :, at + m0:at + m1, :].rearrange("p t m k -> p m t k"),
-                     raw[:, :, PACK * m0:PACK * m1].rearrange("p k (m t) -> p m t k", t=PACK))
-
-        def cast_plain(eng, dst, raw, n0, n1):
-            cast(eng, dst[:, n0:n1, :], raw[:, :, n0:n1].rearrange("p k n -> p n k"))
-
-        def quant(codes, scales, src):
-            nc.vector.quantize_mx(out=codes.bitcast(FP8X4), scales=scales, in_=src)
-
-        def load_rows(name, src, a, c0, c1):
-            raw = tile(name, [P, PACK, c1 - c0], F32)
-            nc.sync.dma_start(out=raw[:], in_=src[a * K_PASS:(a + 1) * K_PASS, c0:c1].rearrange("(p k) w -> p k w", k=PACK))
-            return raw
-
-        w_sc = [tile("w_sc%d" % h, [P, PASSES, HALF], U8) for h in range(2)]
-        w_cols = [(0, HALF), (HALF, HALF + UP_W), (HALF + UP_W, M)]
-        w_wd = [tile("w_wd%d" % i, [P, PASSES, 2 * (n1 - n0)], U8) for i, (n0, n1) in enumerate(w_cols)]
-        for h in range(2):
-            nc.vector.memset(w_sc[h][:].bitcast(I32), 0)
-
-        def load_w_scales(h, queue):
-            for r in range(4):
-                queue.dma_start(
-                    out=w_sc[h][r:P:32, :, :].bitcast(I32),
-                    in_=w4_scales[:, r:16:4, h * HALF:(h + 1) * HALF].rearrange("a q n -> q a n").bitcast(I32),
+        def round_dealt(dst, first, raw):
+            count = raw.shape[2] // PACK
+            cut = vector_share(count, 4)
+            for engine, m0, m1 in ((VECTOR, 0, cut), (SCALAR, cut, count)):
+                round_copy(
+                    engine,
+                    dst[:, :, first + m0:first + m1, :].rearrange("p j m i -> p m i j"),
+                    raw[:, :, PACK * m0:PACK * m1].rearrange("p i (m j) -> p m i j", j=PACK),
                 )
 
-        def load_w_words(i):
-            nc.sync.dma_start(
-                out=w_wd[i][:].bitcast(I32),
-                in_=w4_words[:, :, 2 * w_cols[i][0]:2 * w_cols[i][1]].rearrange("a p b -> p a b").bitcast(I32),
+        def round_plain(engine, dst, raw, n0, n1):
+            round_copy(
+                engine,
+                dst[:, n0:n1, :].rearrange("p (c e) i -> p c i e", e=4),
+                raw[:, :, n0:n1].rearrange("p i (c e) -> p c i e", e=4),
             )
 
-        x_cd = [tile("x_cd%d" % a, [P, T], U32) for a in range(PASSES)]
-        x_sc = [tile("x_sc%d" % a, [P, T], U8) for a in range(PASSES)]
-        d_cd = [tile("d_cd%d" % a, [P, R], U32) for a in range(PASSES)]
-        d_sc = [tile("d_sc%d" % a, [P, R], U8) for a in range(PASSES)]
-        h_cd = [tile("h_cd%d" % c, [P, P], U32) for c in range(PACK)]
-        h_sc = [tile("h_sc%d" % c, [P, P], U8) for c in range(PACK)]
-        u_cd = [tile("u_cd%d" % i, [P, UP_W], U32) for i in range(M // UP_W)]
-        u_sc = [tile("u_sc%d" % i, [P, UP_W], U8) for i in range(M // UP_W)]
-        o_cd = tile("o_cd", [P, M], U32)
-        o_sc = tile("o_sc", [P, M], U8)
+        def quantise(operand, cols, src):
+            words, scales = operand
+            nc.vector.quantize_mx(out=words[:, cols].bitcast(FP8X4), scales=scales[:, cols], in_=src)
 
-        last = PASSES - 1
+        def relu(engine, out, in_):
+            if engine == VECTOR:
+                nc.vector.tensor_scalar(out=out, in0=in_, scalar1=0.0, scalar2=None, op0=ALU.max)
+            else:
+                nc.scalar.activation(out=out, in_=in_, func=ACT.Relu)
+
+        def square(out, in_):
+            nc.scalar.activation(out=out, in_=in_, func=ACT.Square)
+
+
+        def load_rows(name, src, a, cols):
+            raw = sb(name, [P, PACK, cols.stop - cols.start], F32)
+            nc.sync.dma_start(out=raw[:], in_=src[span(a, K_PASS), cols].rearrange("(p i) w -> p i w", i=PACK))
+            return raw
+
+        w_words = [sb("w_words%d" % g, [P, PASSES, 2 * (n1 - n0)], U8) for g, (n0, n1) in enumerate(W_RANGES)]
+        w_scales = [sb("w_scales%d" % g, [P, PASSES, n1 - n0], U8) for g, (n0, n1) in enumerate(W_RANGES)]
+        for scales_tile in w_scales:
+            nc.vector.memset(scales_tile[:].bitcast(I32), 0)
+
+        def load_w_scales(g, queue):
+            n0, n1 = W_RANGES[g]
+            for i in range(4):
+                queue.dma_start(
+                    out=w_scales[g][i:P:QUADRANT, :, :].bitcast(I32),
+                    in_=w4_scales[:, i:SCALE_ROWS:4, n0:n1].rearrange("a q n -> q a n").bitcast(I32),
+                )
+
+        def load_w_words(g):
+            n0, n1 = W_RANGES[g]
+            nc.sync.dma_start(
+                out=w_words[g][:].bitcast(I32),
+                in_=w4_words[:, :, 2 * n0:2 * n1].rearrange("a p b -> p a b").bitcast(I32),
+            )
+
         x_raw = []
-        d_raw = []
-        for a in range(last):
-            x_raw.append(load_rows("x_raw%d" % a, x, a, 0, T))
+        down_raw = []
+        for a in range(LAST_PASS):
+            x_raw.append(load_rows("x_raw%d" % a, x, a, slice(0, T)))
             if a == 0:
                 load_w_scales(0, nc.scalar)
-            d_raw.append(load_rows("d_raw%d" % a, down, a, 0, R))
+            down_raw.append(load_rows("down_raw%d" % a, down, a, slice(0, R)))
             if a == 0:
                 load_w_words(0)
-        x_last = [load_rows("x_last%d" % u, x, last, u * T // 2, (u + 1) * T // 2) for u in range(2)]
-        d_last = [load_rows("d_last%d" % u, down, last, u * R // 2, (u + 1) * R // 2) for u in range(2)]
+        x_halves = [load_rows("x_half%d" % u, x, LAST_PASS, span(u, T // 2)) for u in range(2)]
+        down_halves = [load_rows("down_half%d" % u, down, LAST_PASS, span(u, R // 2)) for u in range(2)]
         load_w_scales(1, nc.sync)
         load_w_words(1)
-        u_raw = []
-        for i in range(M // UP_W):
-            u_raw.append(load_rows("u_raw%d" % i, up, 0, i * UP_W, (i + 1) * UP_W))
-            if i == 1:
-                load_w_words(2)
+        up_raw = [load_rows("up_raw%d" % g, up, 0, span(g, UP_PIECE)) for g in range(3)]
+        load_w_scales(2, nc.sync)
+        load_w_words(2)
+        up_raw.append(load_rows("up_raw3", up, 0, span(3, UP_PIECE)))
 
-        h_ps = [bank(4 + c, "h_ps%d" % c) for c in range(PACK)]
-        y_ps = [bank(b, "y_ps%d" % b) for b in range(4)]
 
-        def col(j):
-            return slice(j * P, (j + 1) * P)
+        x_mx = mx_tiles("x", PASSES, T)
+        down_mx = mx_tiles("down", PASSES, R)
+        h_mx = mx_tiles("h", PACK, P)
+        up_mx = mx_tiles("up", M // UP_PIECE, UP_PIECE)
+        out_mx = mx_tiles("out", 1, M)[0]
+        whole = slice(None)
+
+        def e4m3(operand, cols):
+            words, scales = operand
+            return words[:, cols].bitcast(FP8X4), scales[:, cols]
+
+        def w4_operand(b, a):
+            g = max(i for i in range(len(W_RANGES)) if W_RANGES[i][0] <= b * CHUNK)
+            n0 = b * CHUNK - W_RANGES[g][0]
+            return w_words[g][:, a, 2 * n0:2 * (n0 + CHUNK)].bitcast(FP4X4), w_scales[g][:, a, n0:n0 + CHUNK]
+
+        def up_operand(b):
+            return e4m3(up_mx[b // 2], span(b % 2, CHUNK))
+
+        def matmul(out, stationary, moving, start, stop):
+            nc.tensor.matmul_mx(
+                out=out, lhsT=stationary[0], lhsT_scale=stationary[1], rhs=moving[0], rhs_scale=moving[1], start=start, stop=stop
+            )
+
+        h_acc = [bank(EARLY + c, "h_acc%d" % c, [P, PACK, P]) for c in range(PACK)]
+        y_acc = [bank(b, "y_acc%d" % b, [P, PACK, CHUNK]) for b in range(EARLY)]
 
         def h_pass(a):
             for c in range(PACK):
                 for j in range(PACK):
-                    nc.tensor.matmul_mx(
-                        out=h_ps[c][:, j, :], lhsT=d_cd[a][:, col(j)].bitcast(FP8X4), lhsT_scale=d_sc[a][:, col(j)],
-                        rhs=x_cd[a][:, col(c)].bitcast(FP8X4), rhs_scale=x_sc[a][:, col(c)],
-                        start=(a == 0 and j == 0), stop=(a == last and j == PACK - 1),
+                    matmul(
+                        h_acc[c][:, j, :], e4m3(down_mx[a], span(j, P)), e4m3(x_mx[a], span(c, P)),
+                        start=(a == 0 and j == 0), stop=(a == LAST_PASS and j == PACK - 1),
                     )
 
-        def y_base(b, a):
-            h, n0 = divmod(b * NB, HALF)
-            i = max(i for i in range(len(w_cols)) if w_cols[i][0] <= b * NB)
-            w0 = b * NB - w_cols[i][0]
+        def base_pass(b, a):
             for j in range(PACK):
-                nc.tensor.matmul_mx(
-                    out=y_ps[b][:, j, :], lhsT=x_cd[a][:, col(j)].bitcast(FP8X4), lhsT_scale=x_sc[a][:, col(j)],
-                    rhs=w_wd[i][:, a, 2 * w0:2 * (w0 + NB)].bitcast(FP4X4), rhs_scale=w_sc[h][:, a, n0:n0 + NB],
-                    start=(a == 0 and j == 0), stop=False,
-                )
+                matmul(y_acc[b][:, j, :], e4m3(x_mx[a], span(j, P)), w4_operand(b, a), start=(a == 0 and j == 0), stop=False)
 
-        def late_base(s0, s1):
-            for s in range(s0, s1):
-                b, a = divmod(s, PASSES)
+        def late_base_passes(first, end):
+            for step in range(first, end):
+                late, a = divmod(step, PASSES)
                 if a == 0:
-                    y_ps.append(bank(4 + b, "y_ps%d" % (4 + b)))
-                y_base(4 + b, a)
+                    y_acc.append(bank(EARLY + late, "y_acc%d" % (EARLY + late), [P, PACK, CHUNK]))
+                base_pass(EARLY + late, a)
 
-        def y_up(b):
-            i, n0 = divmod(b * NB, UP_W)
+        def up_pass(b):
             for j in range(PACK):
-                nc.tensor.matmul_mx(
-                    out=y_ps[b][:, j, :], lhsT=h_cd[j][:].bitcast(FP8X4), lhsT_scale=h_sc[j][:],
-                    rhs=u_cd[i][:, n0:n0 + NB].bitcast(FP8X4), rhs_scale=u_sc[i][:, n0:n0 + NB],
-                    start=False, stop=(j == PACK - 1),
-                )
+                matmul(y_acc[b][:, j, :], e4m3(h_mx[j], whole), up_operand(b), start=False, stop=(j == PACK - 1))
 
-        def flat(t):
-            return t[:].rearrange("p t m k -> p (t m k)")
+        def last_chunk_hand(j):
+            acc = bank(j, "y_last%d" % j, [P, CHUNK])
+            for a in range(PASSES):
+                matmul(acc[:], e4m3(x_mx[a], span(j, P)), w4_operand(LAST_CHUNK, a), start=(a == 0), stop=False)
+            matmul(acc[:], e4m3(h_mx[j], whole), up_operand(LAST_CHUNK), start=False, stop=True)
+            return acc
 
-        for a in range(last):
-            xg = tile("xg", [P, PACK, P, PACK], BF16)
-            cast_dealt(xg, 0, x_raw[a], P)
-            quant(x_cd[a][:], x_sc[a][:], flat(xg))
-            for b in range(4):
-                y_base(b, a)
-            dg = tile("dg", [P, PACK, P, PACK], BF16)
-            cast_dealt(dg, 0, d_raw[a], P)
-            if a < last - 1:
-                quant(d_cd[a][:], d_sc[a][:], flat(dg))
+
+        def dealt_tile(name, count):
+            return sb(name, [P, PACK, count, PACK], BF16)
+
+        def merged(dealt):
+            return dealt[:].rearrange("p j m i -> p (j m i)")
+
+        for a in range(LAST_PASS):
+            x_bf = dealt_tile("x_bf", P)
+            round_dealt(x_bf, 0, x_raw[a])
+            quantise(x_mx[a], whole, merged(x_bf))
+            for b in range(EARLY):
+                base_pass(b, a)
+            down_bf = dealt_tile("down_bf", P)
+            round_dealt(down_bf, 0, down_raw[a])
+            if a < LAST_PASS - 1:
+                quantise(down_mx[a], whole, merged(down_bf))
                 h_pass(a)
 
-        xg = tile("xg", [P, PACK, P, PACK], BF16)
-        cast_dealt(xg, 0, x_last[0], P // 2)
-        quant(d_cd[last - 1][:], d_sc[last - 1][:], flat(dg))
-        h_pass(last - 1)
-        cast_dealt(xg, P // 2, x_last[1], P // 2)
-        quant(x_cd[last][:], x_sc[last][:], flat(xg))
-        for b in range(4):
-            y_base(b, last)
+        x_bf = dealt_tile("x_bf", P)
+        round_dealt(x_bf, 0, x_halves[0])
+        quantise(down_mx[LAST_PASS - 1], whole, merged(down_bf))
+        h_pass(LAST_PASS - 1)
+        round_dealt(x_bf, P // 2, x_halves[1])
+        quantise(x_mx[LAST_PASS], whole, merged(x_bf))
+        for b in range(EARLY):
+            base_pass(b, LAST_PASS)
         for u in range(2):
-            g = tile("dl%d" % u, [P, PACK, P // 2, PACK], BF16)
-            cast_dealt(g, 0, d_last[u], P // 2)
+            half_bf = dealt_tile("down_half_bf%d" % u, P // 2)
+            round_dealt(half_bf, 0, down_halves[u])
             for j in range(PACK):
-                cs = slice(j * P + u * P // 2, j * P + (u + 1) * P // 2)
-                quant(d_cd[last][:, cs], d_sc[last][:, cs], g[:, j].rearrange("p m k -> p (m k)"))
-        h_pass(last)
+                quantise(down_mx[LAST_PASS], span(2 * j + u, P // 2), half_bf[:, j].rearrange("p m i -> p (m i)"))
+        h_pass(LAST_PASS)
 
-        ug = [tile("ug%d" % i, [P, UP_W, PACK], BF16) for i in range(M // UP_W)]
-        hg = [tile("hg%d" % c, [P, P, PACK], BF16) for c in range(PACK)]
 
-        def flat3(t):
-            return t[:].rearrange("p n k -> p (n k)")
+        h_bf = [sb("h_bf%d" % c, [P, P, PACK], BF16) for c in range(PACK)]
+        up_bf = [sb("up_bf%d" % g, [P, UP_PIECE, PACK], BF16) for g in range(M // UP_PIECE)]
+        positive = [sb("positive%d" % b, [P, PACK, CHUNK], F32) for b in range(CHUNKS)]
+        result = [sb("result%d" % b, [P, PACK, CHUNK], F32) for b in range(CHUNKS)]
+        result_bf = [sb("result_bf%d" % b, [P, CHUNK, PACK], BF16) for b in range(CHUNKS)]
+        out_rows = out_0.rearrange("(p j) n -> p j n", j=PACK)
+        out_words = out_1.rearrange("a p n i -> p (a n i)").bitcast(I32)
 
-        def h_out(eng, c):
-            cast(eng, hg[c][:], h_ps[c][:].rearrange("p j t -> p t j"))
+        def columns(grouped):
+            return grouped[:].rearrange("p n i -> p (n i)")
 
-        def h_quant(c):
-            quant(h_cd[c][:], h_sc[c][:], flat3(hg[c]))
+        def quantise_h(c):
+            quantise(h_mx[c], whole, columns(h_bf[c]))
 
-        def u_quant(i):
-            quant(u_cd[i][:], u_sc[i][:], flat3(ug[i]))
+        def round_up(g, cut):
+            round_plain(VECTOR, up_bf[g], up_raw[g], 0, cut)
+            if cut < UP_PIECE:
+                round_plain(SCALAR, up_bf[g], up_raw[g], cut, UP_PIECE)
 
-        out0 = out_0.rearrange("(p j) n -> p j n", j=PACK)
-        out1 = out_1.rearrange("a p n i -> p (a n i)").bitcast(I32)
-        rl = {}
-        sq = {}
-        og = {}
+        def quantise_up(g):
+            quantise(up_mx[g], whole, columns(up_bf[g]))
 
-        for b in range(BANKS):
-            rl[b] = tile("rl%d" % b, [P, PACK, NB], F32)
-            sq[b] = tile("sq%d" % b, [P, PACK, NB], F32)
-            og[b] = tile("og%d" % b, [P, NB, PACK], BF16)
+        def store_result(b):
+            nc.sync.dma_start(out=out_rows[:, :, span(b, CHUNK)], in_=result[b][:])
 
-        def relu(eng, b, n0=0, n1=NB):
-            if eng == "v":
-                nc.vector.tensor_scalar(out=rl[b][:, :, n0:n1], in0=y_ps[b][:, :, n0:n1], scalar1=0.0, scalar2=None, op0=ALU.max)
-            else:
-                nc.scalar.activation(out=rl[b][:, :, n0:n1], in_=y_ps[b][:, :, n0:n1], func=ACT.Relu)
+        def square_and_store(b):
+            square(result[b][:], positive[b][:])
+            store_result(b)
 
-        def square(eng, b, n0=0, n1=NB):
-            if eng == "v":
-                nc.vector.tensor_tensor(out=sq[b][:, :, n0:n1], in0=rl[b][:, :, n0:n1], in1=rl[b][:, :, n0:n1], op=ALU.mult)
-            else:
-                nc.scalar.activation(out=sq[b][:, :, n0:n1], in_=rl[b][:, :, n0:n1], func=ACT.Square)
+        def round_result(engine, b):
+            round_plain(engine, result_bf[b], result[b], 0, CHUNK)
 
-        def store_out(b):
-            nc.sync.dma_start(out=out0[:, :, b * NB:(b + 1) * NB], in_=sq[b][:])
+        def quantise_result(b):
+            quantise(out_mx, span(b, CHUNK), columns(result_bf[b]))
 
-        def o_cast(b, n0=0, n1=NB):
-            cast_plain("v", og[b], sq[b], n0, n1)
+        def store_words(b0, b1):
+            cols = slice(b0 * CHUNK, b1 * CHUNK)
+            nc.sync.dma_start(out=out_words[:, cols], in_=out_mx[0][:, cols].bitcast(I32))
 
-        def o_quant(b):
-            quant(o_cd[:, b * NB:(b + 1) * NB], o_sc[:, b * NB:(b + 1) * NB], flat3(og[b]))
+        for c in range(PACK):
+            round_copy(VECTOR if c == 1 else SCALAR, h_bf[c][:], h_acc[c][:].rearrange("p j m -> p m j"))
+        quantise_h(0)
+        quantise_h(1)
+        round_up(0, UP_PIECE)
+        quantise_h(2)
+        quantise_h(3)
+        quantise_up(0)
 
-        def u_cast(i, shared):
-            cut = (2 * UP_W // 3) // 8 * 8 if shared else UP_W
-            cast_plain("v", ug[i], u_raw[i], 0, cut)
-            if shared:
-                cast_plain("s", ug[i], u_raw[i], cut, UP_W)
+        issued = 0
+        for g in range(len(LEAD)):
+            late_base_passes(issued, LEAD[g])
+            issued = LEAD[g]
+            up_pass(2 * g)
+            up_pass(2 * g + 1)
+            round_up(g + 1, vector_share(UP_PIECE, 8) if g == 0 else UP_PIECE)
+            relu(SCALAR, positive[2 * g][:], y_acc[2 * g][:])
+            if g > 0:
+                square_and_store(2 * g - 1)
+                round_result(VECTOR, g - 1)
+            quantise_up(g + 1)
+            relu(VECTOR, positive[2 * g + 1][:], y_acc[2 * g + 1][:])
+            square_and_store(2 * g)
 
-        def store_scales(b0, b1, queues):
-            for r in range(4):
-                queues[r % len(queues)].dma_start(
-                    out=out_2[0, r:16:4, b0 * NB:b1 * NB].bitcast(I32),
-                    in_=o_sc[r:P:32, b0 * NB:b1 * NB].bitcast(I32))
+        late_base_passes(issued, (LAST_CHUNK - EARLY) * PASSES)
+        up_pass(LAST_CHUNK - 1)
+        last_acc = [last_chunk_hand(j) for j in range(PACK)]
+        relu(SCALAR, positive[LAST_CHUNK - 1][:], y_acc[LAST_CHUNK - 1][:])
+        square_and_store(LAST_CHUNK - 2)
+        square_and_store(LAST_CHUNK - 1)
 
-        def store_codes(b0, b1):
-            nc.sync.dma_start(out=out1[:, b0 * NB:b1 * NB], in_=o_cd[:, b0 * NB:b1 * NB].bitcast(I32))
-
-        h_out("s", 0)
-        h_out("v", 1)
-        h_out("s", 2)
-        h_out("s", 3)
-        for c in range(PACK - 1):
-            h_quant(c)
-        u_cast(0, True)
-        h_quant(PACK - 1)
-        u_quant(0)
-        late_base(0, 6)
-        y_up(0)
-        y_up(1)
-        u_cast(1, True)
-        relu("s", 0)
-        u_quant(1)
-        relu("v", 1)
-        late_base(6, 10)
-        y_up(2)
-        y_up(3)
-        square("s", 0)
-        store_out(0)
-        square("s", 1)
-        store_out(1)
-        u_cast(2, False)
-        o_cast(0)
-        u_quant(2)
-        relu("s", 2)
-        relu("s", 3)
-        late_base(10, 13)
-        y_up(4)
-        y_up(5)
-        u_cast(3, False)
-        o_cast(1)
-        u_quant(3)
-        late_base(13, 15)
-        y_up(6)
-        late_base(15, 20)
-        y_up(7)
-        square("s", 2)
-        store_out(2)
-        square("s", 3)
-        store_out(3)
-        relu("v", 4)
-        relu("s", 5)
-        o_quant(0)
-        o_cast(2)
-        o_quant(1)
-        square("s", 4)
-        store_out(4)
-        square("s", 5)
-        store_out(5)
-        o_cast(3)
-        o_quant(2)
-        o_cast(4)
-        o_quant(3)
-        store_codes(0, 4)
-        relu("s", 6)
-        o_cast(5)
-        o_quant(4)
-        end = 7
-        relu("s", end, 0, 64)
-        square("s", 6)
-        store_out(6)
-        relu("s", end, 64, NB)
-        square("v", end, 0, 64)
-        o_quant(5)
-        o_cast(6)
-        square("s", end, 64, NB)
-        store_out(end)
-        o_cast(end, 0, 64)
-        o_quant(6)
-        o_cast(end, 64, NB)
-        store_codes(4, 7)
-        o_quant(end)
-        store_codes(7, 8)
-        store_scales(0, 8, [nc.scalar, nc.sync])
+        quantise_result(0)
+        for j in range(PACK):
+            if j < PACK - 1:
+                round_result(VECTOR, j + 2)
+                quantise_result(j + 1)
+            relu(VECTOR, positive[LAST_CHUNK][:, j, :], last_acc[j][:])
+            square(result[LAST_CHUNK][:, j, :], positive[LAST_CHUNK][:, j, :])
+        store_words(0, 4)
+        store_result(LAST_CHUNK)
+        round_result(SCALAR, 6)
+        round_result(VECTOR, 5)
+        quantise_result(4)
+        round_result(VECTOR, 7)
+        quantise_result(5)
+        store_words(4, 6)
+        quantise_result(6)
+        quantise_result(7)
+        store_words(6, 8)
+        for i in range(4):
+            queue = nc.sync if i % 2 else nc.scalar
+            queue.dma_start(out=out_2[0, i:SCALE_ROWS:4, :].bitcast(I32), in_=out_mx[1][i:P:QUADRANT, :].bitcast(I32))

from contextlib import ExitStack

import concourse.mybir as mybir

K, R, M, T = 2560, 512, 1024, 512
FLOPS = 2 * (K * R * T + K * M * T + R * M * T)

F32 = mybir.dt.float32
BF16 = mybir.dt.bfloat16
I32 = mybir.dt.int32
U32 = mybir.dt.uint32
U8 = mybir.dt.uint8
FP8X4 = mybir.dt.float8_e4m3fn_x4
FP4X4 = mybir.dt.float4_e2m1fn_x4
ACT = mybir.ActivationFunctionType
ALU = mybir.AluOpType

P = 128
PACK = 4
K_PASS = P * PACK
PASSES = K // K_PASS
LAST_PASS = PASSES - 1
QUADRANT = 32
SCALE_ROWS = K_PASS // 32
CHUNK = 128
CHUNKS = M // CHUNK
EARLY = 4
LAST_CHUNK = CHUNKS - 1
UP_PIECE = 2 * CHUNK
W_RANGES = ((0, EARLY * CHUNK), (EARLY * CHUNK, (EARLY + 2) * CHUNK), ((EARLY + 2) * CHUNK, M))
LEAD = (6, 9, 11)
VECTOR, SCALAR = "vector", "scalar"


def vector_share(total, multiple):
    return 2 * total // 3 // multiple * multiple


def tile_mix_lowrank_tm_pl_relu2_kernel(tc, x, w4_words, w4_scales, down, up, out_0, out_1, out_2):
    nc = tc.nc
    with ExitStack() as ctx:
        sbuf = ctx.enter_context(tc.tile_pool(name="sbuf", bufs=1))
        psum = ctx.enter_context(tc.psum_pool(name="psum", bufs=1))
        ctx.enter_context(tc.manual_schedule())

        def sb(name, shape, dtype):
            return sbuf.tile(shape, dtype, name=name, tag=name, align_bytes=64)

        def bank(number, name, shape):
            return psum.tile(shape, F32, name=name, tag="bank%d" % number)

        def mx_tiles(name, count, width):
            return [(sb("%s_words%d" % (name, i), [P, width], U32), sb("%s_scales%d" % (name, i), [P, width], U8)) for i in range(count)]

        def span(i, width):
            return slice(i * width, (i + 1) * width)


        def round_copy(engine, out, in_):
            if engine == VECTOR:
                nc.vector.tensor_copy(out=out, in_=in_)
            else:
                nc.scalar.activation(out=out, in_=in_, func=ACT.Copy)

        def round_dealt(dst, first, raw):
            count = raw.shape[2] // PACK
            cut = vector_share(count, 4)
            for engine, m0, m1 in ((VECTOR, 0, cut), (SCALAR, cut, count)):
                round_copy(
                    engine,
                    dst[:, :, first + m0:first + m1, :].rearrange("p j m i -> p m i j"),
                    raw[:, :, PACK * m0:PACK * m1].rearrange("p i (m j) -> p m i j", j=PACK),
                )

        def round_plain(engine, dst, raw, n0, n1):
            round_copy(
                engine,
                dst[:, n0:n1, :].rearrange("p (c e) i -> p c i e", e=4),
                raw[:, :, n0:n1].rearrange("p i (c e) -> p c i e", e=4),
            )

        def quantise(operand, cols, src):
            words, scales = operand
            nc.vector.quantize_mx(out=words[:, cols].bitcast(FP8X4), scales=scales[:, cols], in_=src)

        def relu(engine, out, in_):
            if engine == VECTOR:
                nc.vector.tensor_scalar(out=out, in0=in_, scalar1=0.0, scalar2=None, op0=ALU.max)
            else:
                nc.scalar.activation(out=out, in_=in_, func=ACT.Relu)

        def square(out, in_):
            nc.scalar.activation(out=out, in_=in_, func=ACT.Square)


        def load_rows(name, src, a, cols):
            raw = sb(name, [P, PACK, cols.stop - cols.start], F32)
            nc.sync.dma_start(out=raw[:], in_=src[span(a, K_PASS), cols].rearrange("(p i) w -> p i w", i=PACK))
            return raw

        w_words = [sb("w_words%d" % g, [P, PASSES, 2 * (n1 - n0)], U8) for g, (n0, n1) in enumerate(W_RANGES)]
        w_scales = [sb("w_scales%d" % g, [P, PASSES, n1 - n0], U8) for g, (n0, n1) in enumerate(W_RANGES)]
        for scales_tile in w_scales:
            nc.vector.memset(scales_tile[:].bitcast(I32), 0)

        def load_w_scales(g, queue):
            n0, n1 = W_RANGES[g]
            for i in range(4):
                queue.dma_start(
                    out=w_scales[g][i:P:QUADRANT, :, :].bitcast(I32),
                    in_=w4_scales[:, i:SCALE_ROWS:4, n0:n1].rearrange("a q n -> q a n").bitcast(I32),
                )

        def load_w_words(g):
            n0, n1 = W_RANGES[g]
            nc.sync.dma_start(
                out=w_words[g][:].bitcast(I32),
                in_=w4_words[:, :, 2 * n0:2 * n1].rearrange("a p b -> p a b").bitcast(I32),
            )

        x_raw = []
        down_raw = []
        for a in range(LAST_PASS):
            x_raw.append(load_rows("x_raw%d" % a, x, a, slice(0, T)))
            if a == 0:
                load_w_scales(0, nc.scalar)
            down_raw.append(load_rows("down_raw%d" % a, down, a, slice(0, R)))
            if a == 0:
                load_w_words(0)
        x_halves = [load_rows("x_half%d" % u, x, LAST_PASS, span(u, T // 2)) for u in range(2)]
        down_halves = [load_rows("down_half%d" % u, down, LAST_PASS, span(u, R // 2)) for u in range(2)]
        load_w_scales(1, nc.sync)
        load_w_words(1)
        up_raw = [load_rows("up_raw%d" % g, up, 0, span(g, UP_PIECE)) for g in range(3)]
        load_w_scales(2, nc.sync)
        load_w_words(2)
        up_raw.append(load_rows("up_raw3", up, 0, span(3, UP_PIECE)))


        x_mx = mx_tiles("x", PASSES, T)
        down_mx = mx_tiles("down", PASSES, R)
        h_mx = mx_tiles("h", PACK, P)
        up_mx = mx_tiles("up", M // UP_PIECE, UP_PIECE)
        out_mx = mx_tiles("out", 1, M)[0]
        whole = slice(None)

        def e4m3(operand, cols):
            words, scales = operand
            return words[:, cols].bitcast(FP8X4), scales[:, cols]

        def w4_operand(b, a):
            g = max(i for i in range(len(W_RANGES)) if W_RANGES[i][0] <= b * CHUNK)
            n0 = b * CHUNK - W_RANGES[g][0]
            return w_words[g][:, a, 2 * n0:2 * (n0 + CHUNK)].bitcast(FP4X4), w_scales[g][:, a, n0:n0 + CHUNK]

        def up_operand(b):
            return e4m3(up_mx[b // 2], span(b % 2, CHUNK))

        def matmul(out, stationary, moving, start, stop):
            nc.tensor.matmul_mx(
                out=out, lhsT=stationary[0], lhsT_scale=stationary[1], rhs=moving[0], rhs_scale=moving[1], start=start, stop=stop
            )

        h_acc = [bank(EARLY + c, "h_acc%d" % c, [P, PACK, P]) for c in range(PACK)]
        y_acc = [bank(b, "y_acc%d" % b, [P, PACK, CHUNK]) for b in range(EARLY)]

        def h_pass(a):
            for c in range(PACK):
                for j in range(PACK):
                    matmul(
                        h_acc[c][:, j, :], e4m3(down_mx[a], span(j, P)), e4m3(x_mx[a], span(c, P)),
                        start=(a == 0 and j == 0), stop=(a == LAST_PASS and j == PACK - 1),
                    )

        def base_pass(b, a):
            for j in range(PACK):
                matmul(y_acc[b][:, j, :], e4m3(x_mx[a], span(j, P)), w4_operand(b, a), start=(a == 0 and j == 0), stop=False)

        def late_base_passes(first, end):
            for step in range(first, end):
                late, a = divmod(step, PASSES)
                if a == 0:
                    y_acc.append(bank(EARLY + late, "y_acc%d" % (EARLY + late), [P, PACK, CHUNK]))
                base_pass(EARLY + late, a)

        def up_pass(b):
            for j in range(PACK):
                matmul(y_acc[b][:, j, :], e4m3(h_mx[j], whole), up_operand(b), start=False, stop=(j == PACK - 1))

        def last_chunk_hand(j):
            acc = bank(j, "y_last%d" % j, [P, CHUNK])
            for a in range(PASSES):
                matmul(acc[:], e4m3(x_mx[a], span(j, P)), w4_operand(LAST_CHUNK, a), start=(a == 0), stop=False)
            matmul(acc[:], e4m3(h_mx[j], whole), up_operand(LAST_CHUNK), start=False, stop=True)
            return acc


        def dealt_tile(name, count):
            return sb(name, [P, PACK, count, PACK], BF16)

        def merged(dealt):
            return dealt[:].rearrange("p j m i -> p (j m i)")

        for a in range(LAST_PASS):
            x_bf = dealt_tile("x_bf", P)
            round_dealt(x_bf, 0, x_raw[a])
            quantise(x_mx[a], whole, merged(x_bf))
            for b in range(EARLY):
                base_pass(b, a)
            down_bf = dealt_tile("down_bf", P)
            round_dealt(down_bf, 0, down_raw[a])
            if a < LAST_PASS - 1:
                quantise(down_mx[a], whole, merged(down_bf))
                h_pass(a)

        x_bf = dealt_tile("x_bf", P)
        round_dealt(x_bf, 0, x_halves[0])
        quantise(down_mx[LAST_PASS - 1], whole, merged(down_bf))
        h_pass(LAST_PASS - 1)
        round_dealt(x_bf, P // 2, x_halves[1])
        quantise(x_mx[LAST_PASS], whole, merged(x_bf))
        for b in range(EARLY):
            base_pass(b, LAST_PASS)
        for u in range(2):
            half_bf = dealt_tile("down_half_bf%d" % u, P // 2)
            round_dealt(half_bf, 0, down_halves[u])
            for j in range(PACK):
                quantise(down_mx[LAST_PASS], span(2 * j + u, P // 2), half_bf[:, j].rearrange("p m i -> p (m i)"))
        h_pass(LAST_PASS)


        h_bf = [sb("h_bf%d" % c, [P, P, PACK], BF16) for c in range(PACK)]
        up_bf = [sb("up_bf%d" % g, [P, UP_PIECE, PACK], BF16) for g in range(M // UP_PIECE)]
        positive = [sb("positive%d" % b, [P, PACK, CHUNK], F32) for b in range(CHUNKS)]
        result = [sb("result%d" % b, [P, PACK, CHUNK], F32) for b in range(CHUNKS)]
        result_bf = [sb("result_bf%d" % b, [P, CHUNK, PACK], BF16) for b in range(CHUNKS)]
        out_rows = out_0.rearrange("(p j) n -> p j n", j=PACK)
        out_words = out_1.rearrange("a p n i -> p (a n i)").bitcast(I32)

        def columns(grouped):
            return grouped[:].rearrange("p n i -> p (n i)")

        def quantise_h(c):
            quantise(h_mx[c], whole, columns(h_bf[c]))

        def round_up(g, cut):
            round_plain(VECTOR, up_bf[g], up_raw[g], 0, cut)
            if cut < UP_PIECE:
                round_plain(SCALAR, up_bf[g], up_raw[g], cut, UP_PIECE)

        def quantise_up(g):
            quantise(up_mx[g], whole, columns(up_bf[g]))

        def store_result(b):
            nc.sync.dma_start(out=out_rows[:, :, span(b, CHUNK)], in_=result[b][:])

        def square_and_store(b):
            square(result[b][:], positive[b][:])
            store_result(b)

        def round_result(engine, b):
            round_plain(engine, result_bf[b], result[b], 0, CHUNK)

        def quantise_result(b):
            quantise(out_mx, span(b, CHUNK), columns(result_bf[b]))

        def store_words(b0, b1):
            cols = slice(b0 * CHUNK, b1 * CHUNK)
            nc.sync.dma_start(out=out_words[:, cols], in_=out_mx[0][:, cols].bitcast(I32))

        for c in range(PACK):
            round_copy(VECTOR if c == 1 else SCALAR, h_bf[c][:], h_acc[c][:].rearrange("p j m -> p m j"))
        quantise_h(0)
        quantise_h(1)
        round_up(0, UP_PIECE)
        quantise_h(2)
        quantise_h(3)
        quantise_up(0)

        issued = 0
        for g in range(len(LEAD)):
            late_base_passes(issued, LEAD[g])
            issued = LEAD[g]
            up_pass(2 * g)
            up_pass(2 * g + 1)
            round_up(g + 1, vector_share(UP_PIECE, 8) if g == 0 else UP_PIECE)
            relu(SCALAR, positive[2 * g][:], y_acc[2 * g][:])
            if g > 0:
                square_and_store(2 * g - 1)
                round_result(VECTOR, g - 1)
            quantise_up(g + 1)
            relu(VECTOR, positive[2 * g + 1][:], y_acc[2 * g + 1][:])
            square_and_store(2 * g)

        late_base_passes(issued, (LAST_CHUNK - EARLY) * PASSES)
        up_pass(LAST_CHUNK - 1)
        last_acc = [last_chunk_hand(j) for j in range(PACK)]
        relu(SCALAR, positive[LAST_CHUNK - 1][:], y_acc[LAST_CHUNK - 1][:])
        square_and_store(LAST_CHUNK - 2)
        square_and_store(LAST_CHUNK - 1)

        quantise_result(0)
        for j in range(PACK):
            if j < PACK - 1:
                round_result(VECTOR, j + 2)
                quantise_result(j + 1)
            relu(VECTOR, positive[LAST_CHUNK][:, j, :], last_acc[j][:])
            square(result[LAST_CHUNK][:, j, :], positive[LAST_CHUNK][:, j, :])
        store_words(0, 4)
        store_result(LAST_CHUNK)
        round_result(SCALAR, 6)
        round_result(VECTOR, 5)
        quantise_result(4)
        round_result(VECTOR, 7)
        quantise_result(5)
        store_words(4, 6)
        quantise_result(6)
        quantise_result(7)
        store_words(6, 8)
        for i in range(4):
            queue = nc.sync if i % 2 else nc.scalar
            queue.dma_start(out=out_2[0, i:SCALE_ROWS:4, :].bitcast(I32), in_=out_mx[1][i:P:QUADRANT, :].bitcast(I32))
